import numpy as np
import ml_dtypes


def mxq(x, axis, fmt="e4m3"):
    dtype, down = {"e4m3": (ml_dtypes.float8_e4m3fn, 7), "e5m2": (ml_dtypes.float8_e5m2, 14)}[fmt]
    v = np.moveaxis(np.asarray(x, np.float32).astype(ml_dtypes.bfloat16).astype(np.float64), axis, -1)
    blocks = v.reshape(v.shape[:-1] + (-1, 32))
    amax = np.abs(blocks).max(-1, keepdims=True)
    byte = np.maximum(np.where(amax > 0, np.frexp(amax)[1] - 1 + 127, 0) - down, 1)
    scale = np.exp2(byte - 127.0)
    codes = (blocks / scale).astype(np.float32).astype(dtype).astype(np.float64)
    return np.moveaxis((codes * scale).reshape(v.shape), -1, axis)


WIDE = False


def mx_kscale(k):
    if not WIDE:
        return np.ones(k)
    levels = np.array([10, -10, 5, -5, 0])
    if k % 512:
        return np.exp2(np.random.permutation(np.resize(levels, k // 32))).repeat(32)
    a = np.empty((k // 512, 16))
    for p in range(k // 512):
        a[p, :8] = np.random.permutation(np.resize(levels, 8))
        for g in range(8):
            far = levels[np.abs(levels - a[p, g]) >= 10]
            a[p, g + 8] = far[np.random.randint(len(far))]
    return np.exp2(a.ravel()).repeat(32)


BF16 = ml_dtypes.bfloat16


def bf(x):
    return np.asarray(x, np.float32).astype(BF16)


def f64(x):
    return np.asarray(x).astype(np.float64)


T, N, K, R = 2048, 1024, 1536, 512
TAU = 2.0
BETA = 0.9


def setup_inputs():
    s, u, t = mx_kscale(T), mx_kscale(N), mx_kscale(K)
    return {"dy": bf(np.random.standard_normal((T, N)) / np.sqrt(T) * s[:, None]),
            "x": bf(np.random.standard_normal((T, K)) / s[:, None]),
            "acc": bf(0.5 * np.random.standard_normal((N, K))),
            "row_gain": bf((1.0 + 0.1 * np.random.standard_normal(N)) * u),
            "col_gain": bf((1.0 + 0.1 * np.random.standard_normal(K)) * t),
            "p": bf(np.random.standard_normal((N, R)) / np.sqrt(N) / u[:, None]),
            "q": bf(np.random.standard_normal((K, R)) / np.sqrt(K) / t[:, None]),
            "v_left": bf(np.random.uniform(0.5, 1.5, (R, K)) * t ** 2),
            "v_right": bf(np.random.uniform(0.5, 1.5, (N, R)) * (u ** 2)[:, None])}


def rms_step(z, v):
    return z / np.sqrt(BETA * v + (1.0 - BETA) * z * z)


def reference(dy, x, acc, row_gain, col_gain, p, q, v_left, v_right):
    d = mxq(f64(dy), 0, "e4m3").T @ mxq(f64(x), 0, "e4m3")
    c = TAU * np.tanh((d + f64(acc)) / TAU)
    g = c * f64(row_gain)[:, None] * f64(col_gain)[None, :]
    left = mxq(f64(p), 0, "e4m3").T @ mxq(g, 0, "e4m3")
    right = mxq(g, 1, "e4m3") @ mxq(f64(q), 0, "e4m3")
    return rms_step(left, f64(v_left)), rms_step(right, f64(v_right))

@@ -1,0 +1,437 @@
+import math
+from contextlib import ExitStack
+
+import concourse.mybir as mybir
+from concourse.masks import make_identity
+
+F32 = mybir.dt.float32
+BF16 = mybir.dt.bfloat16
+U32 = mybir.dt.uint32
+U8 = mybir.dt.uint8
+FP8X4 = mybir.dt.float8_e4m3fn_x4
+ALU = mybir.AluOpType
+ACTF = mybir.ActivationFunctionType
+
+T, N, K, R = 2048, 1024, 1536, 512
+P = 128
+W = 512
+TC = T // W
+NG = N // W
+KB = K // W
+RB = R // P
+
+OPT = {"FH": (("x", 0, 1, "D"), ("x", 1, 1, "D")), "F1": {0: (("x", 2, 1, "A"), ("x", 3, 1, "A")), 1: (), 2: (("q", 1, 0, "A"),), 3: (), 4: (("q", 2, 0, "A"),), 5: ()}, "F2": {0: (), 1: (("x", 1, 2, "A"), ("x", 0, 2, "A")), 2: (), 3: (("p", 1, 0, "A"),), 4: (), 5: ()}, "DSQ": (0, 2, 5, 10, 17), "DMO": (2, 3, 5, 6, 7, 10, 12, 13, 18), "JB": (0, 1, 2, 3, 6, 7, 0, 1, 2, 3, 4, 5, 6, 7, 0, 1, 2, 3, 4, 5), "lags": (1, 2, 3), "steps": {"6": 1, "4a": 0, "4b": 1, "4c": 0, "5a": 1, "5b": 1, "5c": 4}, "PW": {"A4": ("q", 0, 0), "C0": ("x", 2, 2), "C1": ("p", 0, 0), "A2": ("x", 3, 2)}}
+FLOPS = 2 * T * N * K + 2 * (2 * N * K * R)
+
+BANKS = ("d0", "d1", "d2", "d3", "x0", "x1", "x2", "x3")
+
+
+def tile_left_right_projected_grad_f6_kernel(
+    tc, dy, x, acc, row_gain, col_gain, p, q, v_left, v_right, out_0, out_1
+):
+    nc = tc.nc
+    dy_v = dy.rearrange("(c p j) n -> c p j n", p=P, j=4)
+    x_v = x.rearrange("(c p j) k -> c p j k", p=P, j=4)
+    acc_v = acc.rearrange("(g p j) k -> g p j k", p=P, j=4)
+    p_v = p.rearrange("(g p j) r -> g p j r", p=P, j=4)
+    q_v = q.rearrange("(g p j) r -> g p j r", p=P, j=4)
+    vl_v = v_left.rearrange("(b m) k -> m b k", m=P)
+    vr_v = v_right.rearrange("(g p j) r -> g p j r", p=P, j=4)
+    o0_v = out_0.rearrange("(b m) k -> b m k", m=P)
+    o1_v = out_1.rearrange("(g p j) r -> g p j r", p=P, j=4)
+
+    with ExitStack() as ctx:
+        keep = ctx.enter_context(tc.tile_pool(name="keep", bufs=1))
+        rawp = ctx.enter_context(tc.tile_pool(name="rawp", bufs=11))
+        accp = ctx.enter_context(tc.tile_pool(name="accp", bufs=3))
+        stg = ctx.enter_context(tc.tile_pool(name="stg", bufs=5))
+        two = ctx.enter_context(tc.tile_pool(name="two", bufs=2))
+        fin = ctx.enter_context(tc.tile_pool(name="fin", bufs=6))
+        psum = ctx.enter_context(tc.psum_pool(name="psum", bufs=1))
+
+        ident = keep.tile([P, P], F32, name="ident")
+        rg = keep.tile([P, N], BF16, name="rg")
+        cg = keep.tile([P, K], BF16, name="cg")
+        warm = keep.tile([P, 1], F32, name="warm")
+
+        raw = {}
+        npool = [0]
+        blk = {}
+        codes = {}
+
+        src = {}
+        for c in range(TC):
+            for g in range(NG):
+                src["dy", c, g] = dy_v[c][:, :, g * W : (g + 1) * W]
+            for b in range(KB):
+                src["x", c, b] = x_v[c][:, :, b * W : (b + 1) * W]
+        for g in range(NG):
+            src["p", g, 0] = p_v[g]
+            src["vr", g, 0] = vr_v[g]
+        for b in range(KB):
+            src["q", b, 0] = q_v[b]
+            src["vl", b, 0] = vl_v[:, :, b * W : (b + 1) * W]
+
+        def load(key):
+            t = rawp.tile([P, 4, W], BF16, name="raw_%s%d%d" % key, tag="raw", align_bytes=64)
+            raw[key] = t
+            nc.sync.dma_start(out=t[:], in_=src[key])
+
+        def load_acc(u):
+            kb, g = divmod(u, NG)
+            t = accp.tile([P, 4, W], BF16, name="acc%d" % u, tag="acc", align_bytes=64)
+            raw["acc", u] = t
+            nc.sync.dma_start(out=t[:], in_=acc_v[g][:, :, kb * W : (kb + 1) * W])
+
+        def lay(key, engine):
+            if engine == "P" or key in (("x", 1, 1), ("x", 3, 1)):
+                t = keep.tile([P, W, 4], BF16, name="pst_%s%d%d" % key, tag="pst%d" % (npool[0] % 2), align_bytes=64)
+                npool[0] += 1
+            else:
+                t = stg.tile([P, W, 4], BF16, name="stg_%s%d%d" % key, tag="stg", align_bytes=64)
+            blk[key] = t
+            if key[0] == "dy":
+                dst = t[:].rearrange("p (j m) t -> p j m t", j=4)
+                s = raw[key][:].rearrange("p t (m j) -> p j m t", j=4)
+            else:
+                dst = t[:].rearrange("p (c i) t -> p c t i", i=4)
+                s = raw[key][:].rearrange("p t (c i) -> p c t i", i=4)
+            if engine == "D":
+                nc.vector.tensor_copy(out=dst, in_=s)
+            elif engine == "A":
+                nc.scalar.copy(out=dst, in_=s)
+            else:
+                nc.gpsimd.tensor_scalar(out=dst, in0=s, scalar1=1.0, scalar2=0.0, op0=ALU.mult, op1=ALU.add)
+
+        def quant(key, t):
+            cw = keep.tile([P, W], U32, name="c_%s%d%d" % key, align_bytes=64)
+            sc = keep.tile([P, W], U8, name="s_%s%d%d" % key, align_bytes=64)
+            codes[key] = (cw, sc)
+            nc.vector.quantize_mx(
+                out=cw[:].bitcast(FP8X4), scales=sc[:], in_=t[:].rearrange("p w t -> p (w t)")
+            )
+
+        def mx(out, lk, c0, rk, start, stop):
+            lc, ls = codes[lk]
+            rc, rs = codes[rk]
+            nc.tensor.matmul_mx(
+                out=out,
+                lhsT=lc[:, c0 : c0 + P].bitcast(FP8X4),
+                lhsT_scale=ls[:, c0 : c0 + P],
+                rhs=rc[:].bitcast(FP8X4),
+                rhs_scale=rs[:],
+                start=start,
+                stop=stop,
+            )
+
+        def bank(i, nm):
+            return psum.tile([P, W], F32, name=nm, tag=BANKS[i])
+
+        ORDER = (2, 3, 0, 1)
+        d = {}
+        th = {}
+        gbank = {}
+        gt_ = {}
+
+        def d_open(u):
+            d[u] = [bank(j, "d%d_%d" % (u, j)) for j in range(4)]
+
+        def d_pass(u, j, c):
+            kb, g = divmod(u, NG)
+            mx(d[u][j][:], ("dy", c, g), j * P, ("x", c, kb), c == 0, c == TC - 1)
+
+        def d_all(u):
+            d[u] = []
+            for j in range(4):
+                d[u].append(bank(j, "d%d_%d" % (u, j)))
+                for c in range(TC):
+                    d_pass(u, j, c)
+
+        def add(u):
+            t = two.tile([P, 4, W], F32, name="th%d" % u, tag="th", align_bytes=64)
+            th[u] = t
+            for j in range(4):
+                nc.vector.tensor_tensor(
+                    out=t[:, j, :], in0=d[u][j][:], in1=raw["acc", u][:, j, :], op=ALU.add
+                )
+
+        def tanh(u):
+            for h in range(2):
+                s = th[u][:, 2 * h : 2 * h + 2, :]
+                nc.scalar.activation(out=s, in_=s, func=ACTF.Tanh, scale=0.5)
+
+        def gain(u, qd):
+            kb, g = divmod(u, NG)
+            b = psum.tile([P, 4, P], F32, name="g%d_%d" % (u, qd), tag=BANKS[4 + qd])
+            gbank[u, qd] = b
+            k0 = kb * W + qd * P
+            for j in range(4):
+                nc.tensor.matmul(
+                    out=b[:, j, :],
+                    lhsT=rg[:, g * W + j : (g + 1) * W : 4],
+                    rhs=cg[:, k0 : k0 + P],
+                    start=True,
+                    stop=True,
+                )
+
+        def mult(u, qd):
+            if qd == ORDER[0]:
+                gt_[u] = two.tile([P, W, 4], BF16, name="G%d" % u, tag="G", align_bytes=64)
+            ks = slice(qd * P, (qd + 1) * P)
+            nc.vector.tensor_tensor(
+                out=gt_[u][:, ks, :].rearrange("p (c i) j -> p c j i", i=4),
+                in0=th[u][:, :, ks].rearrange("p j (c i) -> p c j i", i=4),
+                in1=gbank[u, qd][:].rearrange("p j (c i) -> p c j i", i=4),
+                op=ALU.mult,
+            )
+
+        tb = {}
+        gtt = {}
+
+        def turn(u):
+            gv = gt_[u][:].rearrange("p k j -> p (k j)").bitcast(F32)
+            gv = gv.rearrange("p (m e w) -> p m e w", e=4, w=2)
+            for w in range(2):
+                b = psum.tile([P, 4, P], F32, name="t%d_%d" % (u, w), tag=BANKS[4 + w])
+                tb[u, w] = b
+                for e in range(4):
+                    nc.tensor.transpose(b[:, e, :], gv[:, :, e, w], ident[:])
+
+        def turn_out(u):
+            gtt[u] = two.tile([P, W, 4], BF16, name="GT%d" % u, tag="GT", align_bytes=64)
+            for w in range(2):
+                nc.scalar.copy(
+                    out=gtt[u][:, 2 * P * w : 2 * P * (w + 1), :].rearrange("m (b p) e -> m b p e", b=2),
+                    in_=tb[u, w][:].bitcast(BF16).rearrange("m e (p b) -> m b p e", b=2),
+                )
+
+        def q_left(u):
+            kb, g = divmod(u, NG)
+            quant(("gl", kb, g), gt_[u])
+
+        def q_right(u):
+            kb, g = divmod(u, NG)
+            quant(("gr", kb, g), gtt[u])
+
+        nc.gpsimd.memset(warm[:], 0.0)
+        nc.scalar.activation(out=warm[:], in_=warm[:], func=ACTF.Tanh)
+        nc.gpsimd.memset(rg[:], 0.0)
+        nc.gpsimd.dma_start(out=rg[0:2, :], in_=row_gain.partition_broadcast(2))
+        nc.gpsimd.memset(cg[:], 0.0)
+        nc.gpsimd.dma_start(out=cg[0:2, :], in_=col_gain.partition_broadcast(2))
+        make_identity(nc, ident[:])
+
+        with tc.manual_schedule():
+            for c in range(TC):
+                load(("dy", c, 0))
+                load(("x", c, 0))
+            load_acc(0)
+
+            d_open(0)
+            for c in range(TC):
+                lay(("dy", c, 0), "D")
+                lay(("x", c, 0), "A")
+                load(("dy", c, 1))
+                if c > 0:
+                    quant(("x", c - 1, 0), blk["x", c - 1, 0])
+                quant(("dy", c, 0), blk["dy", c, 0])
+                if c > 0:
+                    for j in range(4):
+                        d_pass(0, j, c - 1)
+            load_acc(1)
+            for c in range(TC):
+                load(("x", c, 1))
+            lay(("dy", 0, 1), "D")
+            lay(("dy", 1, 1), "A")
+            quant(("x", 3, 0), blk["x", 3, 0])
+            for j in range(4):
+                d_pass(0, j, 3)
+            for qd in range(4):
+                gain(0, ORDER[qd])
+            quant(("dy", 0, 1), blk["dy", 0, 1])
+            lay(("dy", 2, 1), "D")
+            lay(("dy", 3, 1), "A")
+            quant(("dy", 1, 1), blk["dy", 1, 1])
+            add(0)
+            tanh(0)
+            quant(("dy", 2, 1), blk["dy", 2, 1])
+            quant(("dy", 3, 1), blk["dy", 3, 1])
+            d_all(1)
+            for c in range(TC):
+                load(("x", c, 2))
+            load_acc(2)
+
+            FH = OPT["FH"]
+            F1 = OPT["F1"]
+            F2 = OPT["F2"]
+
+            def lays(items, engine):
+                for it in items:
+                    if it[3] == engine:
+                        lay(it[:3], engine)
+
+            def quants(items):
+                for it in items:
+                    quant(it[:3], blk[it[:3]])
+
+            jobs = [("l", b, r) for b in range(KB - 1) for r in range(RB)]
+            jobs += [("r", 0, j) for j in range(4)] + [("l", KB - 1, r) for r in range(RB)]
+            jobs += [("r", 1, j) for j in range(4)]
+            zs = {}
+            fs = {}
+
+            def second(i):
+                kind, a, b = jobs[i]
+                z = bank(JB[i], "z%d" % i)
+                zs[i] = z
+                if kind == "l":
+                    for g in range(NG):
+                        mx(z[:], ("p", g, 0), b * P, ("gl", a, g), g == 0, g == NG - 1)
+                else:
+                    for kb in range(KB):
+                        mx(z[:], ("gr", kb, a), b * P, ("q", kb, 0), kb == 0, kb == KB - 1)
+
+            def vtile(i):
+                kind, a, b = jobs[i]
+                return raw["vl", a, 0][:, b, :] if kind == "l" else raw["vr", a, 0][:, b, :]
+
+            def square(i):
+                f = stg.tile([P, W], F32, name="f%d" % i, tag="stg", align_bytes=64)
+                fs[i] = f
+                if i in DSQ:
+                    zc = fin.tile([P, W], F32, name="zc%d" % i, tag="o", align_bytes=64)
+                    nc.vector.tensor_copy(out=zc[:], in_=zs[i][:])
+                    nc.vector.scalar_tensor_tensor(
+                        out=f[:], in0=zs[i][:], scalar=1.0 / 9.0, in1=zc[:], op0=ALU.mult, op1=ALU.mult
+                    )
+                else:
+                    nc.scalar.activation(out=f[:], in_=zs[i][:], func=ACTF.Square, scale=1.0 / 3.0)
+
+            def moment(i):
+                f = fs[i]
+                eng = nc.vector if i in DMO else nc.gpsimd
+                eng.tensor_tensor(out=f[:], in0=f[:], in1=vtile(i), op=ALU.add)
+
+            def root(i):
+                f = fs[i]
+                nc.scalar.activation(out=f[:], in_=f[:], func=ACTF.Abs_reciprocal_sqrt, scale=0.9)
+
+            def close(i):
+                kind, a, b = jobs[i]
+                o = fin.tile([P, W], F32, name="o%d" % i, tag="o", align_bytes=64)
+                nc.vector.tensor_tensor(out=o[:], in0=zs[i][:], in1=fs[i][:], op=ALU.mult)
+                if kind == "l":
+                    dst = o0_v[b][:, a * W : (a + 1) * W]
+                else:
+                    dst = o1_v[a][:, b, :]
+                nc.sync.dma_start(out=dst, in_=o[:])
+
+            n = len(jobs)
+            last = NG * KB - 1
+            DSQ = OPT["DSQ"]
+            DMO = OPT["DMO"]
+            JB = OPT["JB"]
+
+            LM, LR, LC = OPT["lags"]
+            pos = [0]
+
+            def go(name):
+                c = OPT["steps"][name]
+                steps(pos[0], pos[0] + c)
+                pos[0] += c
+
+            def front(i):
+                second(i)
+                square(i)
+
+            def steps(lo, hi):
+                for i in range(lo, hi):
+                    if i < n:
+                        front(i)
+                    if 0 <= i - LM < n:
+                        moment(i - LM)
+                    if 0 <= i - LR < n:
+                        root(i - LR)
+                    if 0 <= i - LC < n:
+                        close(i - LC)
+
+            PW = OPT["PW"]
+
+            def pwin(name):
+                widx[0] += 1
+                while pending[0] and pending[0][0][1] <= widx[0] - 2:
+                    key = pending[0].pop(0)[0]
+                    quant(key, blk[key])
+                if name in PW:
+                    key = PW[name]
+                    lay(key, "P")
+                    pending[0].append((key, widx[0]))
+
+            pending = [[]]
+            widx = [0]
+            lays(FH, "A")
+            lays(FH, "D")
+            quants(FH)
+            lays(F1[0], "A")
+            for u in range(last + 1):
+                if u + 1 <= last:
+                    pwin("A%d" % (u + 1))
+                    add(u + 1)
+                lays(F1[u], "D")
+                lays(F2[u], "A")
+                if u > 0:
+                    turn_out(u - 1)
+                if u + 1 <= last:
+                    tanh(u + 1)
+                if u + 1 <= last:
+                    lays(F1[u + 1], "A")
+                quants(F1[u])
+                if u == 0:
+                    load_acc(3)
+                    for key in (("p", 0, 0), ("p", 1, 0), ("q", 0, 0), ("q", 1, 0)):
+                        load(key)
+                if u == 2:
+                    for key in (("q", 2, 0), ("vl", 0, 0), ("vl", 1, 0), ("vl", 2, 0)):
+                        load(key)
+                if u == 3:
+                    for key in (("vr", 0, 0), ("vr", 1, 0)):
+                        load(key)
+                if u in (1, 2):
+                    load_acc(u + 3)
+                if u > 0:
+                    gain(u, ORDER[2])
+                    gain(u, ORDER[3])
+                if u + 2 <= last:
+                    d_all(u + 2)
+                if u == last:
+                    while pending[0]:
+                        key = pending[0].pop(0)[0]
+                        quant(key, blk[key])
+                if u == last - 1:
+                    go("4a")
+                if u == last:
+                    go("5a")
+                pwin("C%d" % u)
+                for qd in range(4):
+                    mult(u, ORDER[qd])
+                lays(F2[u], "D")
+                if u == last - 1:
+                    go("4b")
+                if u == last:
+                    go("5b")
+                q_left(u)
+                if u > 0:
+                    q_right(u - 1)
+                turn(u)
+                quants(F2[u])
+                if u == last - 1:
+                    go("4c")
+                if u == last:
+                    go("5c")
+                if u + 1 <= last:
+                    gain(u + 1, ORDER[0])
+                    gain(u + 1, ORDER[1])
+            turn_out(last)
+            go("6")
+            q_right(last)
+            steps(pos[0], n + LC)

@@ -20,7 +20,7 @@ NG = N // W
 KB = K // W
 RB = R // P
 
-OPT = {"FH": (("x", 0, 1, "D"), ("x", 1, 1, "D")), "F1": {0: (("x", 2, 1, "A"), ("x", 3, 1, "A")), 1: (), 2: (("q", 1, 0, "A"),), 3: (), 4: (("q", 2, 0, "A"),), 5: ()}, "F2": {0: (), 1: (("x", 1, 2, "A"), ("x", 0, 2, "A")), 2: (), 3: (("p", 1, 0, "A"),), 4: (), 5: ()}, "DSQ": (0, 2, 5, 10, 17), "DMO": (2, 3, 5, 6, 7, 10, 12, 13, 18), "JB": (0, 1, 2, 3, 6, 7, 0, 1, 2, 3, 4, 5, 6, 7, 0, 1, 2, 3, 4, 5), "lags": (1, 2, 3), "steps": {"6": 1, "4a": 0, "4b": 1, "4c": 0, "5a": 1, "5b": 1, "5c": 4}, "PW": {"A4": ("q", 0, 0), "C0": ("x", 2, 2), "C1": ("p", 0, 0), "A2": ("x", 3, 2)}}
+OPT = {"FH": (("x", 0, 1, "D"), ("x", 1, 1, "D")), "F1": {0: (("x", 2, 1, "M"), ("x", 3, 1, "M")), 1: (("x", 1, 2, "A"), ("x", 2, 2, "A")), 2: (), 3: (), 4: (("q", 1, 0, "A"),), 5: ()}, "F2": {0: (), 1: (), 2: (), 3: (), 4: (), 5: ()}, "DSQ": (0, 1, 4), "DMO": (4, 5, 6, 7, 8, 9, 11, 13, 14, 15, 19), "JB": (0, 1, 2, 3, 6, 7, 0, 1, 2, 3, 4, 5, 6, 7, 0, 1, 2, 3, 4, 5), "lags": (1, 2, 3), "steps": {"6": 2, "4a": 0, "4b": 2, "4c": 0, "5a": 0, "5b": 4, "5c": 0}, "PW": {"A2": ("x", 3, 2), "A5": ("q", 2, 0), "C0": ("x", 0, 2), "C4": ("q", 0, 0), "C3": ("p", 0, 0), "A3": ("p", 1, 0)}, "act": ("TC", "L2", "TH", "L1"), "qpos": (0, 1), "gj": 2, "hq": 1, "ap": 1, "dy1": "ADAA", "x0": "MAMM"}
 FLOPS = 2 * T * N * K + 2 * (2 * N * K * R)
 
 BANKS = ("d0", "d1", "d2", "d3", "x0", "x1", "x2", "x3")
@@ -42,45 +42,47 @@ def tile_left_right_projected_grad_f6_kernel(
 
     with ExitStack() as ctx:
         keep = ctx.enter_context(tc.tile_pool(name="keep", bufs=1))
-        rawp = ctx.enter_context(tc.tile_pool(name="rawp", bufs=11))
-        accp = ctx.enter_context(tc.tile_pool(name="accp", bufs=3))
+        rawp = ctx.enter_context(tc.tile_pool(name="rawp", bufs=12))
+        accp = ctx.enter_context(tc.tile_pool(name="accp", bufs=2))
         stg = ctx.enter_context(tc.tile_pool(name="stg", bufs=5))
         two = ctx.enter_context(tc.tile_pool(name="two", bufs=2))
-        fin = ctx.enter_context(tc.tile_pool(name="fin", bufs=6))
+        fin = ctx.enter_context(tc.tile_pool(name="fin", bufs=4))
         psum = ctx.enter_context(tc.psum_pool(name="psum", bufs=1))
 
         ident = keep.tile([P, P], F32, name="ident")
+        ident_b = keep.tile([P, P], BF16, name="ident_b")
         rg = keep.tile([P, N], BF16, name="rg")
         cg = keep.tile([P, K], BF16, name="cg")
         warm = keep.tile([P, 1], F32, name="warm")
 
         raw = {}
         npool = [0]
+        nmm = [0]
         blk = {}
         codes = {}
 
-        src = {}
-        for c in range(TC):
-            for g in range(NG):
-                src["dy", c, g] = dy_v[c][:, :, g * W : (g + 1) * W]
-            for b in range(KB):
-                src["x", c, b] = x_v[c][:, :, b * W : (b + 1) * W]
-        for g in range(NG):
-            src["p", g, 0] = p_v[g]
-            src["vr", g, 0] = vr_v[g]
-        for b in range(KB):
-            src["q", b, 0] = q_v[b]
-            src["vl", b, 0] = vl_v[:, :, b * W : (b + 1) * W]
+        def put(key, t, src):
+            nc.sync.dma_start(out=t, in_=src)
 
-        def load(key):
-            t = rawp.tile([P, 4, W], BF16, name="raw_%s%d%d" % key, tag="raw", align_bytes=64)
-            raw[key] = t
-            nc.sync.dma_start(out=t[:], in_=src[key])
+        def load_x(c, b):
+            t = rawp.tile([P, 4, W], BF16, name="x%d_%d" % (c, b), tag="raw", align_bytes=64)
+            raw["x", c, b] = t[:]
+            nc.sync.dma_start(out=t[:], in_=x_v[c][:, :, b * W : (b + 1) * W])
+
+        def load_dy(c, g):
+            t = rawp.tile([P, 4, W], BF16, name="dy%d_%d" % (c, g), tag="raw", align_bytes=64)
+            raw["dy", c, g] = t[:]
+            nc.sync.dma_start(out=t[:], in_=dy_v[c][:, :, g * W : (g + 1) * W])
+
+        def load_one(nm, i, src):
+            t = rawp.tile([P, 4, W], BF16, name="%s%d" % (nm, i), tag="raw", align_bytes=64)
+            raw[nm, i, 0] = t[:]
+            nc.sync.dma_start(out=t[:], in_=src)
 
         def load_acc(u):
             kb, g = divmod(u, NG)
             t = accp.tile([P, 4, W], BF16, name="acc%d" % u, tag="acc", align_bytes=64)
-            raw["acc", u] = t
+            raw["acc", u] = t[:]
             nc.sync.dma_start(out=t[:], in_=acc_v[g][:, :, kb * W : (kb + 1) * W])
 
         def lay(key, engine):
@@ -90,16 +92,32 @@ def tile_left_right_projected_grad_f6_kernel(
             else:
                 t = stg.tile([P, W, 4], BF16, name="stg_%s%d%d" % key, tag="stg", align_bytes=64)
             blk[key] = t
+            s0 = raw[key]
             if key[0] == "dy":
-                dst = t[:].rearrange("p (j m) t -> p j m t", j=4)
-                s = raw[key][:].rearrange("p t (m j) -> p j m t", j=4)
+                dst = t[:].rearrange("p (j m) t -> p m t j", j=4)
+                s = raw[key].rearrange("p t (m j) -> p m t j", j=4)
             else:
                 dst = t[:].rearrange("p (c i) t -> p c t i", i=4)
-                s = raw[key][:].rearrange("p t (c i) -> p c t i", i=4)
+                s = raw[key].rearrange("p t (c i) -> p c t i", i=4)
             if engine == "D":
                 nc.vector.tensor_copy(out=dst, in_=s)
             elif engine == "A":
                 nc.scalar.copy(out=dst, in_=s)
+            elif engine == "M":
+                s = s0.rearrange("p t w -> p w t")
+                for h in range(2):
+                    b = psum.tile([P, 2 * P, 4], BF16, name="m_%s%d%d_%d" % (key + (h,)), tag=BANKS[4 + nmm[0] % 4])
+                    nmm[0] += 1
+                    for i in range(2):
+                        c0 = (2 * h + i) * P
+                        nc.tensor.matmul(
+                            out=b[:, i * P : (i + 1) * P, :].rearrange("p c t -> p (c t)"),
+                            lhsT=ident_b[:],
+                            rhs=s[:, c0 : c0 + P, :],
+                            start=True,
+                            stop=True,
+                        )
+                    nc.scalar.copy(out=t[:, 2 * P * h : 2 * P * (h + 1), :], in_=b[:])
             else:
                 nc.gpsimd.tensor_scalar(out=dst, in0=s, scalar1=1.0, scalar2=0.0, op0=ALU.mult, op1=ALU.add)
 
@@ -139,6 +157,13 @@ def tile_left_right_projected_grad_f6_kernel(
         def d_pass(u, j, c):
             kb, g = divmod(u, NG)
             mx(d[u][j][:], ("dy", c, g), j * P, ("x", c, kb), c == 0, c == TC - 1)
+
+        def d_one(u, j):
+            if j == 0:
+                d[u] = []
+            d[u].append(bank(j, "d%d_%d" % (u, j)))
+            for c in range(TC):
+                d_pass(u, j, c)
 
         def d_all(u):
             d[u] = []
@@ -215,6 +240,7 @@ def tile_left_right_projected_grad_f6_kernel(
 
         nc.gpsimd.memset(warm[:], 0.0)
         nc.scalar.activation(out=warm[:], in_=warm[:], func=ACTF.Tanh)
+        make_identity(nc, ident_b[:])
         nc.gpsimd.memset(rg[:], 0.0)
         nc.gpsimd.dma_start(out=rg[0:2, :], in_=row_gain.partition_broadcast(2))
         nc.gpsimd.memset(cg[:], 0.0)
@@ -223,43 +249,52 @@ def tile_left_right_projected_grad_f6_kernel(
 
         with tc.manual_schedule():
             for c in range(TC):
-                load(("dy", c, 0))
-                load(("x", c, 0))
+                load_dy(c, 0)
+                load_x(c, 0)
             load_acc(0)
-
+            for c in range(TC):
+                load_dy(c, 1)
             d_open(0)
             for c in range(TC):
                 lay(("dy", c, 0), "D")
-                lay(("x", c, 0), "A")
-                load(("dy", c, 1))
-                if c > 0:
+                lay(("x", c, 0), OPT["x0"][c])
+                if c > 0 and OPT["hq"] == 1:
                     quant(("x", c - 1, 0), blk["x", c - 1, 0])
-                quant(("dy", c, 0), blk["dy", c, 0])
-                if c > 0:
                     for j in range(4):
                         d_pass(0, j, c - 1)
-            load_acc(1)
-            for c in range(TC):
-                load(("x", c, 1))
-            lay(("dy", 0, 1), "D")
-            lay(("dy", 1, 1), "A")
-            quant(("x", 3, 0), blk["x", 3, 0])
-            for j in range(4):
-                d_pass(0, j, 3)
-            for qd in range(4):
-                gain(0, ORDER[qd])
+                quant(("dy", c, 0), blk["dy", c, 0])
+                if OPT["hq"] == 0:
+                    quant(("x", c, 0), blk["x", c, 0])
+                    for j in range(4):
+                        d_pass(0, j, c)
+                if c == 1:
+                    for i in range(TC):
+                        load_x(i, 1)
+                    load_acc(1)
+            for i in range(TC):
+                load_x(i, 2)
+            lay(("dy", 0, 1), OPT["dy1"][0])
+            lay(("dy", 1, 1), OPT["dy1"][1])
+            if OPT["hq"] == 1:
+                quant(("x", 3, 0), blk["x", 3, 0])
+                for j in range(4):
+                    d_pass(0, j, 3)
             quant(("dy", 0, 1), blk["dy", 0, 1])
-            lay(("dy", 2, 1), "D")
-            lay(("dy", 3, 1), "A")
+            if OPT["ap"] == 0:
+                add(0)
+                tanh(0)
+            lay(("dy", 2, 1), OPT["dy1"][2])
+            lay(("dy", 3, 1), OPT["dy1"][3])
             quant(("dy", 1, 1), blk["dy", 1, 1])
-            add(0)
-            tanh(0)
+            if OPT["ap"] == 1:
+                add(0)
+                tanh(0)
             quant(("dy", 2, 1), blk["dy", 2, 1])
             quant(("dy", 3, 1), blk["dy", 3, 1])
             d_all(1)
-            for c in range(TC):
-                load(("x", c, 2))
             load_acc(2)
+            for g in range(NG):
+                load_one("p", g, p_v[g])
 
             FH = OPT["FH"]
             F1 = OPT["F1"]
@@ -369,40 +404,54 @@ def tile_left_right_projected_grad_f6_kernel(
 
             pending = [[]]
             widx = [0]
+            lays(FH, "M")
+            lays(F1[0], "M")
+            for qd in range(4):
+                gain(0, ORDER[qd])
             lays(FH, "A")
             lays(FH, "D")
             quants(FH)
             lays(F1[0], "A")
             for u in range(last + 1):
-                if u + 1 <= last:
+                if u < last:
                     pwin("A%d" % (u + 1))
                     add(u + 1)
+                for what in OPT["act"]:
+                    if what == "L2":
+                        lays(F2[u], "A")
+                    elif what == "L1" and u < last:
+                        lays(F1[u + 1], "A")
+                    elif what == "TC" and u > 0:
+                        turn_out(u - 1)
+                    elif what == "TH" and u < last:
+                        tanh(u + 1)
                 lays(F1[u], "D")
-                lays(F2[u], "A")
-                if u > 0:
-                    turn_out(u - 1)
-                if u + 1 <= last:
-                    tanh(u + 1)
-                if u + 1 <= last:
-                    lays(F1[u + 1], "A")
+                if OPT["qpos"][0] == 0 and u > 0:
+                    q_left(u - 1)
                 quants(F1[u])
+                if OPT["qpos"][0] == 1 and u > 0:
+                    q_left(u - 1)
+                if OPT["qpos"][1] == 0 and u > 0:
+                    q_right(u - 1)
                 if u == 0:
                     load_acc(3)
-                    for key in (("p", 0, 0), ("p", 1, 0), ("q", 0, 0), ("q", 1, 0)):
-                        load(key)
+                    load_one("q", 0, q_v[0])
+                    load_one("q", 1, q_v[1])
+                if u == 1:
+                    load_acc(4)
+                    load_one("q", 2, q_v[2])
+                    for b in range(KB):
+                        load_one("vl", b, vl_v[:, :, b * W : (b + 1) * W])
                 if u == 2:
-                    for key in (("q", 2, 0), ("vl", 0, 0), ("vl", 1, 0), ("vl", 2, 0)):
-                        load(key)
-                if u == 3:
-                    for key in (("vr", 0, 0), ("vr", 1, 0)):
-                        load(key)
-                if u in (1, 2):
-                    load_acc(u + 3)
-                if u > 0:
-                    gain(u, ORDER[2])
-                    gain(u, ORDER[3])
-                if u + 2 <= last:
-                    d_all(u + 2)
+                    load_acc(5)
+                    for g in range(NG):
+                        load_one("vr", g, vr_v[g])
+                for j in range(4):
+                    if j == OPT["gj"] and u > 0:
+                        gain(u, ORDER[2])
+                        gain(u, ORDER[3])
+                    if u + 2 <= last:
+                        d_one(u + 2, j)
                 if u == last:
                     while pending[0]:
                         key = pending[0].pop(0)[0]
@@ -419,14 +468,14 @@ def tile_left_right_projected_grad_f6_kernel(
                     go("4b")
                 if u == last:
                     go("5b")
-                q_left(u)
-                if u > 0:
+                if OPT["qpos"][1] == 1 and u > 0:
                     q_right(u - 1)
                 turn(u)
                 quants(F2[u])
                 if u == last - 1:
                     go("4c")
                 if u == last:
+                    q_left(u)
                     go("5c")
                 if u + 1 <= last:
                     gain(u + 1, ORDER[0])

@@ -20,7 +20,7 @@ NG = N // W
 KB = K // W
 RB = R // P
 
-OPT = {"FH": (("x", 0, 1, "D"), ("x", 1, 1, "D")), "F1": {0: (("x", 2, 1, "M"), ("x", 3, 1, "M")), 1: (("x", 1, 2, "A"), ("x", 2, 2, "A")), 2: (), 3: (), 4: (("q", 1, 0, "A"),), 5: ()}, "F2": {0: (), 1: (), 2: (), 3: (), 4: (), 5: ()}, "DSQ": (0, 1, 4), "DMO": (4, 5, 6, 7, 8, 9, 11, 13, 14, 15, 19), "JB": (0, 1, 2, 3, 6, 7, 0, 1, 2, 3, 4, 5, 6, 7, 0, 1, 2, 3, 4, 5), "lags": (1, 2, 3), "steps": {"6": 2, "4a": 0, "4b": 2, "4c": 0, "5a": 0, "5b": 4, "5c": 0}, "PW": {"A2": ("x", 3, 2), "A5": ("q", 2, 0), "C0": ("x", 0, 2), "C4": ("q", 0, 0), "C3": ("p", 0, 0), "A3": ("p", 1, 0)}, "act": ("TC", "L2", "TH", "L1"), "qpos": (0, 1), "gj": 2, "hq": 1, "ap": 1, "dy1": "ADAA", "x0": "MAMM"}
+OPT = {"FH": (("x", 0, 1, "M"), ("x", 1, 1, "M")), "F1": {0: (("x", 2, 1, "A"), ("x", 3, 1, "A")), 1: (("x", 3, 2, "A"), ("x", 0, 2, "D")), 2: (("q", 1, 0, "A"),), 3: (), 4: (("q", 2, 0, "A"),), 5: ()}, "F2": {0: (("x", 1, 2, "A"),), 1: (("x", 2, 2, "M"),), 2: (("p", 1, 0, "A"),), 3: (("p", 0, 0, "A"), ("q", 0, 0, "D")), 4: (), 5: ()}, "DSQ": (2, 6, 10), "DMO": (2, 4, 10, 16, 19), "JB": (6, 7, 0, 1, 2, 3, 6, 7, 4, 5, 0, 1, 2, 3, 6, 7, 4, 5, 0, 1), "lags": (1, 2, 3), "steps": {"6": 1, "4a": 0, "4b": 1, "4c": 0, "5a": 1, "5b": 1, "5c": 4}, "PW": {}, "act": ("TC", "L2", "TH", "L1"), "qpos": (1, 1), "gj": 1, "hq": 1, "ap": 0, "d1": 2, "dy1": "DADD", "x0": "AMAA"}
 FLOPS = 2 * T * N * K + 2 * (2 * N * K * R)
 
 BANKS = ("d0", "d1", "d2", "d3", "x0", "x1", "x2", "x3")
@@ -58,6 +58,7 @@ def tile_left_right_projected_grad_f6_kernel(
         raw = {}
         npool = [0]
         nmm = [0]
+        nmb = [4]
         blk = {}
         codes = {}
 
@@ -94,8 +95,8 @@ def tile_left_right_projected_grad_f6_kernel(
             blk[key] = t
             s0 = raw[key]
             if key[0] == "dy":
-                dst = t[:].rearrange("p (j m) t -> p m t j", j=4)
-                s = raw[key].rearrange("p t (m j) -> p m t j", j=4)
+                dst = t[:].rearrange("p (j m) t -> p j m t", j=4)
+                s = raw[key].rearrange("p t (m j) -> p j m t", j=4)
             else:
                 dst = t[:].rearrange("p (c i) t -> p c t i", i=4)
                 s = raw[key].rearrange("p t (c i) -> p c t i", i=4)
@@ -106,7 +107,7 @@ def tile_left_right_projected_grad_f6_kernel(
             elif engine == "M":
                 s = s0.rearrange("p t w -> p w t")
                 for h in range(2):
-                    b = psum.tile([P, 2 * P, 4], BF16, name="m_%s%d%d_%d" % (key + (h,)), tag=BANKS[4 + nmm[0] % 4])
+                    b = psum.tile([P, 2 * P, 4], BF16, name="m_%s%d%d_%d" % (key + (h,)), tag=BANKS[4 + nmm[0] % nmb[0]])
                     nmm[0] += 1
                     for i in range(2):
                         c0 = (2 * h + i) * P
@@ -119,7 +120,7 @@ def tile_left_right_projected_grad_f6_kernel(
                         )
                     nc.scalar.copy(out=t[:, 2 * P * h : 2 * P * (h + 1), :], in_=b[:])
             else:
-                nc.gpsimd.tensor_scalar(out=dst, in0=s, scalar1=1.0, scalar2=0.0, op0=ALU.mult, op1=ALU.add)
+                nc.gpsimd.tensor_scalar(out=t[:], in0=s0.rearrange("p t w -> p w t"), scalar1=1.0, scalar2=0.0, op0=ALU.mult, op1=ALU.add)
 
         def quant(key, t):
             cw = keep.tile([P, W], U32, name="c_%s%d%d" % key, align_bytes=64)
@@ -187,7 +188,7 @@ def tile_left_right_projected_grad_f6_kernel(
 
         def gain(u, qd):
             kb, g = divmod(u, NG)
-            b = psum.tile([P, 4, P], F32, name="g%d_%d" % (u, qd), tag=BANKS[4 + qd])
+            b = psum.tile([P, 4, P], F32, name="g%d_%d" % (u, qd), tag=BANKS[(4 if u < NG * KB - 1 else 0) + qd])
             gbank[u, qd] = b
             k0 = kb * W + qd * P
             for j in range(4):
@@ -291,7 +292,8 @@ def tile_left_right_projected_grad_f6_kernel(
                 tanh(0)
             quant(("dy", 2, 1), blk["dy", 2, 1])
             quant(("dy", 3, 1), blk["dy", 3, 1])
-            d_all(1)
+            if OPT["d1"] == 0:
+                d_all(1)
             load_acc(2)
             for g in range(NG):
                 load_one("p", g, p_v[g])
@@ -405,13 +407,18 @@ def tile_left_right_projected_grad_f6_kernel(
             pending = [[]]
             widx = [0]
             lays(FH, "M")
+            if OPT["d1"] == 1:
+                d_all(1)
             lays(F1[0], "M")
+            if OPT["d1"] == 2:
+                d_all(1)
             for qd in range(4):
                 gain(0, ORDER[qd])
             lays(FH, "A")
             lays(FH, "D")
             quants(FH)
             lays(F1[0], "A")
+            nmb[0] = 2
             for u in range(last + 1):
                 if u < last:
                     pwin("A%d" % (u + 1))
@@ -419,8 +426,10 @@ def tile_left_right_projected_grad_f6_kernel(
                 for what in OPT["act"]:
                     if what == "L2":
                         lays(F2[u], "A")
+                        lays(F2[u], "M")
                     elif what == "L1" and u < last:
                         lays(F1[u + 1], "A")
+                        lays(F1[u + 1], "M")
                     elif what == "TC" and u > 0:
                         turn_out(u - 1)
                     elif what == "TH" and u < last:
@@ -447,11 +456,14 @@ def tile_left_right_projected_grad_f6_kernel(
                     for g in range(NG):
                         load_one("vr", g, vr_v[g])
                 for j in range(4):
-                    if j == OPT["gj"] and u > 0:
+                    if j == OPT["gj"] and 0 < u < last:
                         gain(u, ORDER[2])
                         gain(u, ORDER[3])
                     if u + 2 <= last:
                         d_one(u + 2, j)
+                if u == last - 1:
+                    for qd in range(4):
+                        gain(last, ORDER[qd])
                 if u == last:
                     while pending[0]:
                         key = pending[0].pop(0)[0]
@@ -477,7 +489,7 @@ def tile_left_right_projected_grad_f6_kernel(
                 if u == last:
                     q_left(u)
                     go("5c")
-                if u + 1 <= last:
+                if u + 1 < last:
                     gain(u + 1, ORDER[0])
                     gain(u + 1, ORDER[1])
             turn_out(last)

@@ -20,7 +20,7 @@ NG = N // W
 KB = K // W
 RB = R // P
 
-OPT = {"FH": (("x", 0, 1, "M"), ("x", 1, 1, "M")), "F1": {0: (("x", 2, 1, "A"), ("x", 3, 1, "A")), 1: (("x", 3, 2, "A"), ("x", 0, 2, "D")), 2: (("q", 1, 0, "A"),), 3: (), 4: (("q", 2, 0, "A"),), 5: ()}, "F2": {0: (("x", 1, 2, "A"),), 1: (("x", 2, 2, "M"),), 2: (("p", 1, 0, "A"),), 3: (("p", 0, 0, "A"), ("q", 0, 0, "D")), 4: (), 5: ()}, "DSQ": (2, 6, 10), "DMO": (2, 4, 10, 16, 19), "JB": (6, 7, 0, 1, 2, 3, 6, 7, 4, 5, 0, 1, 2, 3, 6, 7, 4, 5, 0, 1), "lags": (1, 2, 3), "steps": {"6": 1, "4a": 0, "4b": 1, "4c": 0, "5a": 1, "5b": 1, "5c": 4}, "PW": {}, "act": ("TC", "L2", "TH", "L1"), "qpos": (1, 1), "gj": 1, "hq": 1, "ap": 0, "d1": 2, "dy1": "DADD", "x0": "AMAA"}
+OPT = {'FH': [('x', 0, 1, 'D'), ('x', 1, 1, 'D')], 'F1': {0: [('x', 2, 1, 'A'), ('x', 3, 1, 'A')], 1: [('x', 3, 2, 'A')], 2: [], 3: [], 4: [('p', 1, 0, 'A')], 5: []}, 'F2': {0: [('x', 0, 2, 'A')], 1: [('x', 1, 2, 'A')], 2: [('q', 2, 0, 'A')], 3: [], 4: [], 5: []}, 'DSQ': [2, 7, 9, 15], 'DMO': [2, 9, 11, 16, 19], 'JB': [6, 7, 0, 1, 2, 3, 6, 7, 0, 1, 2, 3, 4, 5, 6, 7, 0, 1, 2, 3], 'lags': [2, 2, 4], 'steps': {'6': 6, '4a': 0, '4b': 1, '4c': 0, '5a': 1, '5b': 5, '5c': 0}, 'dy0': 'DDDM', 'dy1': 'ADDA', 'x0': 'ADAM', 'act': ['TC', 'L2', 'TH', 'L1'], 'd1': 0, 'hq': 0, 'ap': 1, 'qpos': [1, 1], 'gj': 1, 'E': {4: []}, 'early': [1, 1, 3, 4], 'accpos': 2, 'PW': {'C0': (('x', 2, 2), 0), 'A2': (('x', 2, 2), 1), 'C2': (('q', 0, 0), 0), 'C3': (('q', 0, 0), 1), 'C1': (('p', 0, 0), 0), 'A5': (('p', 0, 0), 1), 'A4': (('q', 1, 0), 0), 'C4': (('q', 1, 0), 1)}}
 FLOPS = 2 * T * N * K + 2 * (2 * N * K * R)
 
 BANKS = ("d0", "d1", "d2", "d3", "x0", "x1", "x2", "x3")
@@ -44,9 +44,9 @@ def tile_left_right_projected_grad_f6_kernel(
         keep = ctx.enter_context(tc.tile_pool(name="keep", bufs=1))
         rawp = ctx.enter_context(tc.tile_pool(name="rawp", bufs=12))
         accp = ctx.enter_context(tc.tile_pool(name="accp", bufs=2))
-        stg = ctx.enter_context(tc.tile_pool(name="stg", bufs=5))
+        stg = ctx.enter_context(tc.tile_pool(name="stg", bufs=7))
         two = ctx.enter_context(tc.tile_pool(name="two", bufs=2))
-        fin = ctx.enter_context(tc.tile_pool(name="fin", bufs=4))
+        fin = ctx.enter_context(tc.tile_pool(name="fin", bufs=6))
         psum = ctx.enter_context(tc.psum_pool(name="psum", bufs=1))
 
         ident = keep.tile([P, P], F32, name="ident")
@@ -56,7 +56,6 @@ def tile_left_right_projected_grad_f6_kernel(
         warm = keep.tile([P, 1], F32, name="warm")
 
         raw = {}
-        npool = [0]
         nmm = [0]
         nmb = [4]
         blk = {}
@@ -87,10 +86,7 @@ def tile_left_right_projected_grad_f6_kernel(
             nc.sync.dma_start(out=t[:], in_=acc_v[g][:, :, kb * W : (kb + 1) * W])
 
         def lay(key, engine):
-            if engine == "P" or key in (("x", 1, 1), ("x", 3, 1)):
-                t = keep.tile([P, W, 4], BF16, name="pst_%s%d%d" % key, tag="pst%d" % (npool[0] % 2), align_bytes=64)
-                npool[0] += 1
-            else:
+            if True:
                 t = stg.tile([P, W, 4], BF16, name="stg_%s%d%d" % key, tag="stg", align_bytes=64)
             blk[key] = t
             s0 = raw[key]
@@ -104,26 +100,49 @@ def tile_left_right_projected_grad_f6_kernel(
                 nc.vector.tensor_copy(out=dst, in_=s)
             elif engine == "A":
                 nc.scalar.copy(out=dst, in_=s)
-            elif engine == "M":
-                s = s0.rearrange("p t w -> p w t")
+            elif engine in ("M", "N"):
+                if key[0] == "dy":
+                    pieces = [s0.rearrange("p t (m j) -> p j m t", j=4)[:, c, :, :] for c in range(4)]
+                else:
+                    pieces = [s0.rearrange("p t w -> p w t")[:, c * P : (c + 1) * P, :] for c in range(4)]
                 for h in range(2):
-                    b = psum.tile([P, 2 * P, 4], BF16, name="m_%s%d%d_%d" % (key + (h,)), tag=BANKS[4 + nmm[0] % nmb[0]])
-                    nmm[0] += 1
+                    b = psum.tile([P, 2 * P, 4], BF16, name="m_%s%d%d_%d" % (key + (h,)), tag=BANKS[6 + h if engine == "N" else 4 + nmm[0] % nmb[0]])
+                    if engine == "M":
+                        nmm[0] += 1
                     for i in range(2):
-                        c0 = (2 * h + i) * P
                         nc.tensor.matmul(
                             out=b[:, i * P : (i + 1) * P, :].rearrange("p c t -> p (c t)"),
                             lhsT=ident_b[:],
-                            rhs=s[:, c0 : c0 + P, :],
+                            rhs=pieces[2 * h + i],
                             start=True,
                             stop=True,
                         )
                     nc.scalar.copy(out=t[:, 2 * P * h : 2 * P * (h + 1), :], in_=b[:])
-            else:
-                nc.gpsimd.tensor_scalar(out=t[:], in0=s0.rearrange("p t w -> p w t"), scalar1=1.0, scalar2=0.0, op0=ALU.mult, op1=ALU.add)
+
+        hb = {}
+        H = W // 2
+
+        def lay_half(key, h, kind):
+            t = keep.tile([P, H, 4], BF16, name="ph_%s%d%d" % key + "_%d" % h, tag="ph" + kind, align_bytes=64)
+            hb[key, h] = t
+            nc.gpsimd.tensor_scalar(
+                out=t[:], in0=raw[key][:, :, h * H : (h + 1) * H].rearrange("p t w -> p w t"),
+                scalar1=1.0, scalar2=0.0, op0=ALU.mult, op1=ALU.add,
+            )
+
+        def quant_half(key, h):
+            if key not in codes:
+                cw = keep.tile([P, W], U32, name="c_%s%d%d" % key, tag="c_%s%d%d" % key, align_bytes=64)
+                sc = keep.tile([P, W], U8, name="s_%s%d%d" % key, align_bytes=64)
+                codes[key] = (cw, sc)
+            cw, sc = codes[key]
+            cs = slice(h * H, (h + 1) * H)
+            nc.vector.quantize_mx(
+                out=cw[:, cs].bitcast(FP8X4), scales=sc[:, cs], in_=hb[key, h][:].rearrange("p w t -> p (w t)")
+            )
 
         def quant(key, t):
-            cw = keep.tile([P, W], U32, name="c_%s%d%d" % key, align_bytes=64)
+            cw = keep.tile([P, W], U32, name="c_%s%d%d" % key, tag="c_%s%d%d" % key, align_bytes=64)
             sc = keep.tile([P, W], U8, name="s_%s%d%d" % key, align_bytes=64)
             codes[key] = (cw, sc)
             nc.vector.quantize_mx(
@@ -249,49 +268,64 @@ def tile_left_right_projected_grad_f6_kernel(
         make_identity(nc, ident[:])
 
         with tc.manual_schedule():
+            EARLY = OPT["early"]
+            rest = [i for i in range(TC) if EARLY[i] >= TC]
             for c in range(TC):
                 load_dy(c, 0)
                 load_x(c, 0)
-            load_acc(0)
-            for c in range(TC):
-                load_dy(c, 1)
+                for i in range(TC):
+                    if EARLY[i] == c:
+                        load_dy(i, 1)
+            for k, i in enumerate(rest):
+                if k == OPT["accpos"]:
+                    load_acc(0)
+                load_dy(i, 1)
+            if OPT["accpos"] >= len(rest):
+                load_acc(0)
             d_open(0)
+            wait = []
             for c in range(TC):
-                lay(("dy", c, 0), "D")
+                lay(("dy", c, 0), OPT["dy0"][c])
                 lay(("x", c, 0), OPT["x0"][c])
-                if c > 0 and OPT["hq"] == 1:
+                if c > 0:
                     quant(("x", c - 1, 0), blk["x", c - 1, 0])
                     for j in range(4):
                         d_pass(0, j, c - 1)
                 quant(("dy", c, 0), blk["dy", c, 0])
-                if OPT["hq"] == 0:
-                    quant(("x", c, 0), blk["x", c, 0])
-                    for j in range(4):
-                        d_pass(0, j, c)
+                while wait:
+                    key = wait.pop(0)
+                    quant(key, blk[key])
+                for i in range(TC):
+                    if EARLY[i] == c:
+                        lay(("dy", i, 1), OPT["dy1"][i])
+                        wait.append(("dy", i, 1))
                 if c == 1:
                     for i in range(TC):
                         load_x(i, 1)
                     load_acc(1)
             for i in range(TC):
                 load_x(i, 2)
-            lay(("dy", 0, 1), OPT["dy1"][0])
-            lay(("dy", 1, 1), OPT["dy1"][1])
-            if OPT["hq"] == 1:
-                quant(("x", 3, 0), blk["x", 3, 0])
-                for j in range(4):
-                    d_pass(0, j, 3)
-            quant(("dy", 0, 1), blk["dy", 0, 1])
+            for i in rest[:2]:
+                lay(("dy", i, 1), OPT["dy1"][i])
+                wait.append(("dy", i, 1))
+            quant(("x", 3, 0), blk["x", 3, 0])
+            for j in range(4):
+                d_pass(0, j, 3)
+            if wait:
+                key = wait.pop(0)
+                quant(key, blk[key])
             if OPT["ap"] == 0:
                 add(0)
                 tanh(0)
-            lay(("dy", 2, 1), OPT["dy1"][2])
-            lay(("dy", 3, 1), OPT["dy1"][3])
-            quant(("dy", 1, 1), blk["dy", 1, 1])
+            for i in rest[2:]:
+                lay(("dy", i, 1), OPT["dy1"][i])
+                wait.append(("dy", i, 1))
             if OPT["ap"] == 1:
                 add(0)
                 tanh(0)
-            quant(("dy", 2, 1), blk["dy", 2, 1])
-            quant(("dy", 3, 1), blk["dy", 3, 1])
+            while wait:
+                key = wait.pop(0)
+                quant(key, blk[key])
             if OPT["d1"] == 0:
                 d_all(1)
             load_acc(2)
@@ -315,6 +349,7 @@ def tile_left_right_projected_grad_f6_kernel(
             jobs += [("r", 0, j) for j in range(4)] + [("l", KB - 1, r) for r in range(RB)]
             jobs += [("r", 1, j) for j in range(4)]
             zs = {}
+            zcs = {}
             fs = {}
 
             def second(i):
@@ -337,12 +372,15 @@ def tile_left_right_projected_grad_f6_kernel(
                 fs[i] = f
                 if i in DSQ:
                     zc = fin.tile([P, W], F32, name="zc%d" % i, tag="o", align_bytes=64)
+                    zcs[i] = zc
                     nc.vector.tensor_copy(out=zc[:], in_=zs[i][:])
-                    nc.vector.scalar_tensor_tensor(
-                        out=f[:], in0=zs[i][:], scalar=1.0 / 9.0, in1=zc[:], op0=ALU.mult, op1=ALU.mult
-                    )
                 else:
                     nc.scalar.activation(out=f[:], in_=zs[i][:], func=ACTF.Square, scale=1.0 / 3.0)
+
+            def square2(i):
+                nc.vector.scalar_tensor_tensor(
+                    out=fs[i][:], in0=zs[i][:], scalar=1.0 / 9.0, in1=zcs[i][:], op0=ALU.mult, op1=ALU.mult
+                )
 
             def moment(i):
                 f = fs[i]
@@ -350,6 +388,9 @@ def tile_left_right_projected_grad_f6_kernel(
                 eng.tensor_tensor(out=f[:], in0=f[:], in1=vtile(i), op=ALU.add)
 
             def root(i):
+                if i in due:
+                    due.remove(i)
+                    moment(i)
                 f = fs[i]
                 nc.scalar.activation(out=f[:], in_=f[:], func=ACTF.Abs_reciprocal_sqrt, scale=0.9)
 
@@ -381,31 +422,55 @@ def tile_left_right_projected_grad_f6_kernel(
                 second(i)
                 square(i)
 
+            E = OPT["E"]
+            early = [i for u in E for i in E[u]]
+            due = []
+
+            def early_front(u):
+                for k, i in enumerate(E.get(u, ())):
+                    a, b = jobs[i][1:]
+                    z = bank(6 + k % 2, "z%d" % i)
+                    for g in range(NG):
+                        mx(z[:], ("p", g, 0), b * P, ("gl", a, g), g == 0, g == NG - 1)
+                    zc = keep.tile([P, W], F32, name="zc%d" % i, tag="c_x%d%d" % (b, 2 * a), align_bytes=64)
+                    f = keep.tile([P, W], F32, name="f%d" % i, tag=("c_x%d1" if a == 0 else "c_dy%d0") % b, align_bytes=64)
+                    zs[i] = zc
+                    fs[i] = f
+                    nc.scalar.copy(out=zc[:], in_=z[:])
+                    nc.scalar.activation(out=f[:], in_=z[:], func=ACTF.Square, scale=1.0 / 3.0)
+                    due.append(i)
+
+            def early_moment(k):
+                for i in range(k):
+                    moment(due.pop(0))
+
             def steps(lo, hi):
                 for i in range(lo, hi):
-                    if i < n:
+                    if i < n and i not in early:
                         front(i)
-                    if 0 <= i - LM < n:
+                    if 0 <= i - LM < n and i - LM not in early and (LM > 0 or i not in DSQ):
                         moment(i - LM)
                     if 0 <= i - LR < n:
                         root(i - LR)
                     if 0 <= i - LC < n:
                         close(i - LC)
+                    if i < n and i in DSQ and i not in early:
+                        square2(i)
+                        if LM == 0:
+                            moment(i)
 
             PW = OPT["PW"]
 
             def pwin(name):
-                widx[0] += 1
-                while pending[0] and pending[0][0][1] <= widx[0] - 2:
-                    key = pending[0].pop(0)[0]
-                    quant(key, blk[key])
+                kind = name[0]
+                if pending[kind] is not None:
+                    quant_half(*pending[kind])
+                    pending[kind] = None
                 if name in PW:
-                    key = PW[name]
-                    lay(key, "P")
-                    pending[0].append((key, widx[0]))
+                    pending[kind] = PW[name]
+                    lay_half(PW[name][0], PW[name][1], kind)
 
-            pending = [[]]
-            widx = [0]
+            pending = {"A": None, "C": None}
             lays(FH, "M")
             if OPT["d1"] == 1:
                 d_all(1)
@@ -419,9 +484,11 @@ def tile_left_right_projected_grad_f6_kernel(
             quants(FH)
             lays(F1[0], "A")
             nmb[0] = 2
+            late = []
             for u in range(last + 1):
                 if u < last:
                     pwin("A%d" % (u + 1))
+                    early_moment((len(due) + 1) // 2)
                     add(u + 1)
                 for what in OPT["act"]:
                     if what == "L2":
@@ -438,6 +505,7 @@ def tile_left_right_projected_grad_f6_kernel(
                 if OPT["qpos"][0] == 0 and u > 0:
                     q_left(u - 1)
                 quants(F1[u])
+                quants(late)
                 if OPT["qpos"][0] == 1 and u > 0:
                     q_left(u - 1)
                 if OPT["qpos"][1] == 0 and u > 0:
@@ -465,17 +533,21 @@ def tile_left_right_projected_grad_f6_kernel(
                     for qd in range(4):
                         gain(last, ORDER[qd])
                 if u == last:
-                    while pending[0]:
-                        key = pending[0].pop(0)[0]
-                        quant(key, blk[key])
+                    for kind in ("A", "C"):
+                        if pending[kind] is not None:
+                            quant_half(*pending[kind])
+                            pending[kind] = None
                 if u == last - 1:
                     go("4a")
                 if u == last:
                     go("5a")
                 pwin("C%d" % u)
+                early_moment(len(due))
                 for qd in range(4):
                     mult(u, ORDER[qd])
                 lays(F2[u], "D")
+                lays(F2[u], "N")
+                early_front(u)
                 if u == last - 1:
                     go("4b")
                 if u == last:
@@ -483,7 +555,8 @@ def tile_left_right_projected_grad_f6_kernel(
                 if OPT["qpos"][1] == 1 and u > 0:
                     q_right(u - 1)
                 turn(u)
-                quants(F2[u])
+                quants([it for it in F2[u] if it[3] != "N"])
+                late = [it for it in F2[u] if it[3] == "N"]
                 if u == last - 1:
                     go("4c")
                 if u == last:

import math
from contextlib import ExitStack

import concourse.mybir as mybir
from concourse.masks import make_identity

F32 = mybir.dt.float32
BF16 = mybir.dt.bfloat16
U32 = mybir.dt.uint32
U8 = mybir.dt.uint8
FP8X4 = mybir.dt.float8_e4m3fn_x4
ALU = mybir.AluOpType
ACTF = mybir.ActivationFunctionType

T, N, K, R = 2048, 1024, 1536, 512
P = 128
W = 512
TC = T // W
NG = N // W
KB = K // W
RB = R // P

OPT = {'FH': [('x', 0, 1, 'D'), ('x', 1, 1, 'D')], 'F1': {0: [('x', 2, 1, 'A'), ('x', 3, 1, 'A')], 1: [('x', 3, 2, 'A')], 2: [], 3: [], 4: [('p', 1, 0, 'A')], 5: []}, 'F2': {0: [('x', 0, 2, 'A')], 1: [('x', 1, 2, 'A')], 2: [('q', 2, 0, 'A')], 3: [], 4: [], 5: []}, 'DSQ': [2, 7, 9, 15], 'DMO': [2, 9, 11, 16, 19], 'JB': [6, 7, 0, 1, 2, 3, 6, 7, 0, 1, 2, 3, 4, 5, 6, 7, 0, 1, 2, 3], 'lags': [2, 2, 4], 'steps': {'6': 6, '4a': 0, '4b': 1, '4c': 0, '5a': 1, '5b': 5, '5c': 0}, 'dy0': 'DDDM', 'dy1': 'ADDA', 'x0': 'ADAM', 'act': ['TC', 'L2', 'TH', 'L1'], 'd1': 0, 'hq': 0, 'ap': 1, 'qpos': [1, 1], 'gj': 1, 'E': {4: []}, 'early': [1, 1, 3, 4], 'accpos': 2, 'PW': {'C0': (('x', 2, 2), 0), 'A2': (('x', 2, 2), 1), 'C2': (('q', 0, 0), 0), 'C3': (('q', 0, 0), 1), 'C1': (('p', 0, 0), 0), 'A5': (('p', 0, 0), 1), 'A4': (('q', 1, 0), 0), 'C4': (('q', 1, 0), 1)}}
FLOPS = 2 * T * N * K + 2 * (2 * N * K * R)

BANKS = ("d0", "d1", "d2", "d3", "x0", "x1", "x2", "x3")


def tile_left_right_projected_grad_f6_kernel(
    tc, dy, x, acc, row_gain, col_gain, p, q, v_left, v_right, out_0, out_1
):
    nc = tc.nc
    dy_v = dy.rearrange("(c p j) n -> c p j n", p=P, j=4)
    x_v = x.rearrange("(c p j) k -> c p j k", p=P, j=4)
    acc_v = acc.rearrange("(g p j) k -> g p j k", p=P, j=4)
    p_v = p.rearrange("(g p j) r -> g p j r", p=P, j=4)
    q_v = q.rearrange("(g p j) r -> g p j r", p=P, j=4)
    vl_v = v_left.rearrange("(b m) k -> m b k", m=P)
    vr_v = v_right.rearrange("(g p j) r -> g p j r", p=P, j=4)
    o0_v = out_0.rearrange("(b m) k -> b m k", m=P)
    o1_v = out_1.rearrange("(g p j) r -> g p j r", p=P, j=4)

    with ExitStack() as ctx:
        keep = ctx.enter_context(tc.tile_pool(name="keep", bufs=1))
        rawp = ctx.enter_context(tc.tile_pool(name="rawp", bufs=12))
        accp = ctx.enter_context(tc.tile_pool(name="accp", bufs=2))
        stg = ctx.enter_context(tc.tile_pool(name="stg", bufs=7))
        two = ctx.enter_context(tc.tile_pool(name="two", bufs=2))
        fin = ctx.enter_context(tc.tile_pool(name="fin", bufs=6))
        psum = ctx.enter_context(tc.psum_pool(name="psum", bufs=1))

        ident = keep.tile([P, P], F32, name="ident")
        ident_b = keep.tile([P, P], BF16, name="ident_b")
        rg = keep.tile([P, N], BF16, name="rg")
        cg = keep.tile([P, K], BF16, name="cg")
        warm = keep.tile([P, 1], F32, name="warm")

        raw = {}
        nmm = [0]
        nmb = [4]
        blk = {}
        codes = {}

        def put(key, t, src):
            nc.sync.dma_start(out=t, in_=src)

        def load_x(c, b):
            t = rawp.tile([P, 4, W], BF16, name="x%d_%d" % (c, b), tag="raw", align_bytes=64)
            raw["x", c, b] = t[:]
            nc.sync.dma_start(out=t[:], in_=x_v[c][:, :, b * W : (b + 1) * W])

        def load_dy(c, g):
            t = rawp.tile([P, 4, W], BF16, name="dy%d_%d" % (c, g), tag="raw", align_bytes=64)
            raw["dy", c, g] = t[:]
            nc.sync.dma_start(out=t[:], in_=dy_v[c][:, :, g * W : (g + 1) * W])

        def load_one(nm, i, src):
            t = rawp.tile([P, 4, W], BF16, name="%s%d" % (nm, i), tag="raw", align_bytes=64)
            raw[nm, i, 0] = t[:]
            nc.sync.dma_start(out=t[:], in_=src)

        def load_acc(u):
            kb, g = divmod(u, NG)
            t = accp.tile([P, 4, W], BF16, name="acc%d" % u, tag="acc", align_bytes=64)
            raw["acc", u] = t[:]
            nc.sync.dma_start(out=t[:], in_=acc_v[g][:, :, kb * W : (kb + 1) * W])

        def lay(key, engine):
            if True:
                t = stg.tile([P, W, 4], BF16, name="stg_%s%d%d" % key, tag="stg", align_bytes=64)
            blk[key] = t
            s0 = raw[key]
            if key[0] == "dy":
                dst = t[:].rearrange("p (j m) t -> p j m t", j=4)
                s = raw[key].rearrange("p t (m j) -> p j m t", j=4)
            else:
                dst = t[:].rearrange("p (c i) t -> p c t i", i=4)
                s = raw[key].rearrange("p t (c i) -> p c t i", i=4)
            if engine == "D":
                nc.vector.tensor_copy(out=dst, in_=s)
            elif engine == "A":
                nc.scalar.copy(out=dst, in_=s)
            elif engine in ("M", "N"):
                if key[0] == "dy":
                    pieces = [s0.rearrange("p t (m j) -> p j m t", j=4)[:, c, :, :] for c in range(4)]
                else:
                    pieces = [s0.rearrange("p t w -> p w t")[:, c * P : (c + 1) * P, :] for c in range(4)]
                for h in range(2):
                    b = psum.tile([P, 2 * P, 4], BF16, name="m_%s%d%d_%d" % (key + (h,)), tag=BANKS[6 + h if engine == "N" else 4 + nmm[0] % nmb[0]])
                    if engine == "M":
                        nmm[0] += 1
                    for i in range(2):
                        nc.tensor.matmul(
                            out=b[:, i * P : (i + 1) * P, :].rearrange("p c t -> p (c t)"),
                            lhsT=ident_b[:],
                            rhs=pieces[2 * h + i],
                            start=True,
                            stop=True,
                        )
                    nc.scalar.copy(out=t[:, 2 * P * h : 2 * P * (h + 1), :], in_=b[:])

        hb = {}
        H = W // 2

        def lay_half(key, h, kind):
            t = keep.tile([P, H, 4], BF16, name="ph_%s%d%d" % key + "_%d" % h, tag="ph" + kind, align_bytes=64)
            hb[key, h] = t
            nc.gpsimd.tensor_scalar(
                out=t[:], in0=raw[key][:, :, h * H : (h + 1) * H].rearrange("p t w -> p w t"),
                scalar1=1.0, scalar2=0.0, op0=ALU.mult, op1=ALU.add,
            )

        def quant_half(key, h):
            if key not in codes:
                cw = keep.tile([P, W], U32, name="c_%s%d%d" % key, tag="c_%s%d%d" % key, align_bytes=64)
                sc = keep.tile([P, W], U8, name="s_%s%d%d" % key, align_bytes=64)
                codes[key] = (cw, sc)
            cw, sc = codes[key]
            cs = slice(h * H, (h + 1) * H)
            nc.vector.quantize_mx(
                out=cw[:, cs].bitcast(FP8X4), scales=sc[:, cs], in_=hb[key, h][:].rearrange("p w t -> p (w t)")
            )

        def quant(key, t):
            cw = keep.tile([P, W], U32, name="c_%s%d%d" % key, tag="c_%s%d%d" % key, align_bytes=64)
            sc = keep.tile([P, W], U8, name="s_%s%d%d" % key, align_bytes=64)
            codes[key] = (cw, sc)
            nc.vector.quantize_mx(
                out=cw[:].bitcast(FP8X4), scales=sc[:], in_=t[:].rearrange("p w t -> p (w t)")
            )

        def mx(out, lk, c0, rk, start, stop):
            lc, ls = codes[lk]
            rc, rs = codes[rk]
            nc.tensor.matmul_mx(
                out=out,
                lhsT=lc[:, c0 : c0 + P].bitcast(FP8X4),
                lhsT_scale=ls[:, c0 : c0 + P],
                rhs=rc[:].bitcast(FP8X4),
                rhs_scale=rs[:],
                start=start,
                stop=stop,
            )

        def bank(i, nm):
            return psum.tile([P, W], F32, name=nm, tag=BANKS[i])

        ORDER = (2, 3, 0, 1)
        d = {}
        th = {}
        gbank = {}
        gt_ = {}

        def d_open(u):
            d[u] = [bank(j, "d%d_%d" % (u, j)) for j in range(4)]

        def d_pass(u, j, c):
            kb, g = divmod(u, NG)
            mx(d[u][j][:], ("dy", c, g), j * P, ("x", c, kb), c == 0, c == TC - 1)

        def d_one(u, j):
            if j == 0:
                d[u] = []
            d[u].append(bank(j, "d%d_%d" % (u, j)))
            for c in range(TC):
                d_pass(u, j, c)

        def d_all(u):
            d[u] = []
            for j in range(4):
                d[u].append(bank(j, "d%d_%d" % (u, j)))
                for c in range(TC):
                    d_pass(u, j, c)

        def add(u):
            t = two.tile([P, 4, W], F32, name="th%d" % u, tag="th", align_bytes=64)
            th[u] = t
            for j in range(4):
                nc.vector.tensor_tensor(
                    out=t[:, j, :], in0=d[u][j][:], in1=raw["acc", u][:, j, :], op=ALU.add
                )

        def tanh(u):
            for h in range(2):
                s = th[u][:, 2 * h : 2 * h + 2, :]
                nc.scalar.activation(out=s, in_=s, func=ACTF.Tanh, scale=0.5)

        def gain(u, qd):
            kb, g = divmod(u, NG)
            b = psum.tile([P, 4, P], F32, name="g%d_%d" % (u, qd), tag=BANKS[(4 if u < NG * KB - 1 else 0) + qd])
            gbank[u, qd] = b
            k0 = kb * W + qd * P
            for j in range(4):
                nc.tensor.matmul(
                    out=b[:, j, :],
                    lhsT=rg[:, g * W + j : (g + 1) * W : 4],
                    rhs=cg[:, k0 : k0 + P],
                    start=True,
                    stop=True,
                )

        def mult(u, qd):
            if qd == ORDER[0]:
                gt_[u] = two.tile([P, W, 4], BF16, name="G%d" % u, tag="G", align_bytes=64)
            ks = slice(qd * P, (qd + 1) * P)
            nc.vector.tensor_tensor(
                out=gt_[u][:, ks, :].rearrange("p (c i) j -> p c j i", i=4),
                in0=th[u][:, :, ks].rearrange("p j (c i) -> p c j i", i=4),
                in1=gbank[u, qd][:].rearrange("p j (c i) -> p c j i", i=4),
                op=ALU.mult,
            )

        tb = {}
        gtt = {}

        def turn(u):
            gv = gt_[u][:].rearrange("p k j -> p (k j)").bitcast(F32)
            gv = gv.rearrange("p (m e w) -> p m e w", e=4, w=2)
            for w in range(2):
                b = psum.tile([P, 4, P], F32, name="t%d_%d" % (u, w), tag=BANKS[4 + w])
                tb[u, w] = b
                for e in range(4):
                    nc.tensor.transpose(b[:, e, :], gv[:, :, e, w], ident[:])

        def turn_out(u):
            gtt[u] = two.tile([P, W, 4], BF16, name="GT%d" % u, tag="GT", align_bytes=64)
            for w in range(2):
                nc.scalar.copy(
                    out=gtt[u][:, 2 * P * w : 2 * P * (w + 1), :].rearrange("m (b p) e -> m b p e", b=2),
                    in_=tb[u, w][:].bitcast(BF16).rearrange("m e (p b) -> m b p e", b=2),
                )

        def q_left(u):
            kb, g = divmod(u, NG)
            quant(("gl", kb, g), gt_[u])

        def q_right(u):
            kb, g = divmod(u, NG)
            quant(("gr", kb, g), gtt[u])

        nc.gpsimd.memset(warm[:], 0.0)
        nc.scalar.activation(out=warm[:], in_=warm[:], func=ACTF.Tanh)
        make_identity(nc, ident_b[:])
        nc.gpsimd.memset(rg[:], 0.0)
        nc.gpsimd.dma_start(out=rg[0:2, :], in_=row_gain.partition_broadcast(2))
        nc.gpsimd.memset(cg[:], 0.0)
        nc.gpsimd.dma_start(out=cg[0:2, :], in_=col_gain.partition_broadcast(2))
        make_identity(nc, ident[:])

        with tc.manual_schedule():
            EARLY = OPT["early"]
            rest = [i for i in range(TC) if EARLY[i] >= TC]
            for c in range(TC):
                load_dy(c, 0)
                load_x(c, 0)
                for i in range(TC):
                    if EARLY[i] == c:
                        load_dy(i, 1)
            for k, i in enumerate(rest):
                if k == OPT["accpos"]:
                    load_acc(0)
                load_dy(i, 1)
            if OPT["accpos"] >= len(rest):
                load_acc(0)
            d_open(0)
            wait = []
            for c in range(TC):
                lay(("dy", c, 0), OPT["dy0"][c])
                lay(("x", c, 0), OPT["x0"][c])
                if c > 0:
                    quant(("x", c - 1, 0), blk["x", c - 1, 0])
                    for j in range(4):
                        d_pass(0, j, c - 1)
                quant(("dy", c, 0), blk["dy", c, 0])
                while wait:
                    key = wait.pop(0)
                    quant(key, blk[key])
                for i in range(TC):
                    if EARLY[i] == c:
                        lay(("dy", i, 1), OPT["dy1"][i])
                        wait.append(("dy", i, 1))
                if c == 1:
                    for i in range(TC):
                        load_x(i, 1)
                    load_acc(1)
            for i in range(TC):
                load_x(i, 2)
            for i in rest[:2]:
                lay(("dy", i, 1), OPT["dy1"][i])
                wait.append(("dy", i, 1))
            quant(("x", 3, 0), blk["x", 3, 0])
            for j in range(4):
                d_pass(0, j, 3)
            if wait:
                key = wait.pop(0)
                quant(key, blk[key])
            if OPT["ap"] == 0:
                add(0)
                tanh(0)
            for i in rest[2:]:
                lay(("dy", i, 1), OPT["dy1"][i])
                wait.append(("dy", i, 1))
            if OPT["ap"] == 1:
                add(0)
                tanh(0)
            while wait:
                key = wait.pop(0)
                quant(key, blk[key])
            if OPT["d1"] == 0:
                d_all(1)
            load_acc(2)
            for g in range(NG):
                load_one("p", g, p_v[g])

            FH = OPT["FH"]
            F1 = OPT["F1"]
            F2 = OPT["F2"]

            def lays(items, engine):
                for it in items:
                    if it[3] == engine:
                        lay(it[:3], engine)

            def quants(items):
                for it in items:
                    quant(it[:3], blk[it[:3]])

            jobs = [("l", b, r) for b in range(KB - 1) for r in range(RB)]
            jobs += [("r", 0, j) for j in range(4)] + [("l", KB - 1, r) for r in range(RB)]
            jobs += [("r", 1, j) for j in range(4)]
            zs = {}
            zcs = {}
            fs = {}

            def second(i):
                kind, a, b = jobs[i]
                z = bank(JB[i], "z%d" % i)
                zs[i] = z
                if kind == "l":
                    for g in range(NG):
                        mx(z[:], ("p", g, 0), b * P, ("gl", a, g), g == 0, g == NG - 1)
                else:
                    for kb in range(KB):
                        mx(z[:], ("gr", kb, a), b * P, ("q", kb, 0), kb == 0, kb == KB - 1)

            def vtile(i):
                kind, a, b = jobs[i]
                return raw["vl", a, 0][:, b, :] if kind == "l" else raw["vr", a, 0][:, b, :]

            def square(i):
                f = stg.tile([P, W], F32, name="f%d" % i, tag="stg", align_bytes=64)
                fs[i] = f
                if i in DSQ:
                    zc = fin.tile([P, W], F32, name="zc%d" % i, tag="o", align_bytes=64)
                    zcs[i] = zc
                    nc.vector.tensor_copy(out=zc[:], in_=zs[i][:])
                else:
                    nc.scalar.activation(out=f[:], in_=zs[i][:], func=ACTF.Square, scale=1.0 / 3.0)

            def square2(i):
                nc.vector.scalar_tensor_tensor(
                    out=fs[i][:], in0=zs[i][:], scalar=1.0 / 9.0, in1=zcs[i][:], op0=ALU.mult, op1=ALU.mult
                )

            def moment(i):
                f = fs[i]
                eng = nc.vector if i in DMO else nc.gpsimd
                eng.tensor_tensor(out=f[:], in0=f[:], in1=vtile(i), op=ALU.add)

            def root(i):
                if i in due:
                    due.remove(i)
                    moment(i)
                f = fs[i]
                nc.scalar.activation(out=f[:], in_=f[:], func=ACTF.Abs_reciprocal_sqrt, scale=0.9)

            def close(i):
                kind, a, b = jobs[i]
                o = fin.tile([P, W], F32, name="o%d" % i, tag="o", align_bytes=64)
                nc.vector.tensor_tensor(out=o[:], in0=zs[i][:], in1=fs[i][:], op=ALU.mult)
                if kind == "l":
                    dst = o0_v[b][:, a * W : (a + 1) * W]
                else:
                    dst = o1_v[a][:, b, :]
                nc.sync.dma_start(out=dst, in_=o[:])

            n = len(jobs)
            last = NG * KB - 1
            DSQ = OPT["DSQ"]
            DMO = OPT["DMO"]
            JB = OPT["JB"]

            LM, LR, LC = OPT["lags"]
            pos = [0]

            def go(name):
                c = OPT["steps"][name]
                steps(pos[0], pos[0] + c)
                pos[0] += c

            def front(i):
                second(i)
                square(i)

            E = OPT["E"]
            early = [i for u in E for i in E[u]]
            due = []

            def early_front(u):
                for k, i in enumerate(E.get(u, ())):
                    a, b = jobs[i][1:]
                    z = bank(6 + k % 2, "z%d" % i)
                    for g in range(NG):
                        mx(z[:], ("p", g, 0), b * P, ("gl", a, g), g == 0, g == NG - 1)
                    zc = keep.tile([P, W], F32, name="zc%d" % i, tag="c_x%d%d" % (b, 2 * a), align_bytes=64)
                    f = keep.tile([P, W], F32, name="f%d" % i, tag=("c_x%d1" if a == 0 else "c_dy%d0") % b, align_bytes=64)
                    zs[i] = zc
                    fs[i] = f
                    nc.scalar.copy(out=zc[:], in_=z[:])
                    nc.scalar.activation(out=f[:], in_=z[:], func=ACTF.Square, scale=1.0 / 3.0)
                    due.append(i)

            def early_moment(k):
                for i in range(k):
                    moment(due.pop(0))

            def steps(lo, hi):
                for i in range(lo, hi):
                    if i < n and i not in early:
                        front(i)
                    if 0 <= i - LM < n and i - LM not in early and (LM > 0 or i not in DSQ):
                        moment(i - LM)
                    if 0 <= i - LR < n:
                        root(i - LR)
                    if 0 <= i - LC < n:
                        close(i - LC)
                    if i < n and i in DSQ and i not in early:
                        square2(i)
                        if LM == 0:
                            moment(i)

            PW = OPT["PW"]

            def pwin(name):
                kind = name[0]
                if pending[kind] is not None:
                    quant_half(*pending[kind])
                    pending[kind] = None
                if name in PW:
                    pending[kind] = PW[name]
                    lay_half(PW[name][0], PW[name][1], kind)

            pending = {"A": None, "C": None}
            lays(FH, "M")
            if OPT["d1"] == 1:
                d_all(1)
            lays(F1[0], "M")
            if OPT["d1"] == 2:
                d_all(1)
            for qd in range(4):
                gain(0, ORDER[qd])
            lays(FH, "A")
            lays(FH, "D")
            quants(FH)
            lays(F1[0], "A")
            nmb[0] = 2
            late = []
            for u in range(last + 1):
                if u < last:
                    pwin("A%d" % (u + 1))
                    early_moment((len(due) + 1) // 2)
                    add(u + 1)
                for what in OPT["act"]:
                    if what == "L2":
                        lays(F2[u], "A")
                        lays(F2[u], "M")
                    elif what == "L1" and u < last:
                        lays(F1[u + 1], "A")
                        lays(F1[u + 1], "M")
                    elif what == "TC" and u > 0:
                        turn_out(u - 1)
                    elif what == "TH" and u < last:
                        tanh(u + 1)
                lays(F1[u], "D")
                if OPT["qpos"][0] == 0 and u > 0:
                    q_left(u - 1)
                quants(F1[u])
                quants(late)
                if OPT["qpos"][0] == 1 and u > 0:
                    q_left(u - 1)
                if OPT["qpos"][1] == 0 and u > 0:
                    q_right(u - 1)
                if u == 0:
                    load_acc(3)
                    load_one("q", 0, q_v[0])
                    load_one("q", 1, q_v[1])
                if u == 1:
                    load_acc(4)
                    load_one("q", 2, q_v[2])
                    for b in range(KB):
                        load_one("vl", b, vl_v[:, :, b * W : (b + 1) * W])
                if u == 2:
                    load_acc(5)
                    for g in range(NG):
                        load_one("vr", g, vr_v[g])
                for j in range(4):
                    if j == OPT["gj"] and 0 < u < last:
                        gain(u, ORDER[2])
                        gain(u, ORDER[3])
                    if u + 2 <= last:
                        d_one(u + 2, j)
                if u == last - 1:
                    for qd in range(4):
                        gain(last, ORDER[qd])
                if u == last:
                    for kind in ("A", "C"):
                        if pending[kind] is not None:
                            quant_half(*pending[kind])
                            pending[kind] = None
                if u == last - 1:
                    go("4a")
                if u == last:
                    go("5a")
                pwin("C%d" % u)
                early_moment(len(due))
                for qd in range(4):
                    mult(u, ORDER[qd])
                lays(F2[u], "D")
                lays(F2[u], "N")
                early_front(u)
                if u == last - 1:
                    go("4b")
                if u == last:
                    go("5b")
                if OPT["qpos"][1] == 1 and u > 0:
                    q_right(u - 1)
                turn(u)
                quants([it for it in F2[u] if it[3] != "N"])
                late = [it for it in F2[u] if it[3] == "N"]
                if u == last - 1:
                    go("4c")
                if u == last:
                    q_left(u)
                    go("5c")
                if u + 1 < last:
                    gain(u + 1, ORDER[0])
                    gain(u + 1, ORDER[1])
            turn_out(last)
            go("6")
            q_right(last)
            steps(pos[0], n + LC)
